import numpy as np
import ml_dtypes


def mxq(x, axis, fmt="e4m3"):
    dtype, down = {"e4m3": (ml_dtypes.float8_e4m3fn, 7), "e5m2": (ml_dtypes.float8_e5m2, 14)}[fmt]
    v = np.moveaxis(np.asarray(x, np.float32).astype(ml_dtypes.bfloat16).astype(np.float64), axis, -1)
    blocks = v.reshape(v.shape[:-1] + (-1, 32))
    amax = np.abs(blocks).max(-1, keepdims=True)
    byte = np.maximum(np.where(amax > 0, np.frexp(amax)[1] - 1 + 127, 0) - down, 1)
    scale = np.exp2(byte - 127.0)
    codes = (blocks / scale).astype(np.float32).astype(dtype).astype(np.float64)
    return np.moveaxis((codes * scale).reshape(v.shape), -1, axis)


WIDE = False


def mx_kscale(k):
    if not WIDE:
        return np.ones(k)
    levels = np.array([10, -10, 5, -5, 0])
    if k % 512:
        return np.exp2(np.random.permutation(np.resize(levels, k // 32))).repeat(32)
    a = np.empty((k // 512, 16))
    for p in range(k // 512):
        a[p, :8] = np.random.permutation(np.resize(levels, 8))
        for g in range(8):
            far = levels[np.abs(levels - a[p, g]) >= 10]
            a[p, g + 8] = far[np.random.randint(len(far))]
    return np.exp2(a.ravel()).repeat(32)


def f64(x):
    return np.asarray(x).astype(np.float64)


def striped(idx):
    return np.tile(np.asarray(idx).reshape(-1, 16).T, (8, 1)).astype(np.uint16)


def unstriped(offs):
    return offs[:16].T.reshape(-1).astype(np.int64)


def striped8(idx):
    return np.asarray(idx).reshape(8, -1, 16).transpose(0, 2, 1).reshape(128, -1).astype(np.uint16)


def unstriped8(offs):
    return offs.reshape(8, 16, -1).transpose(0, 2, 1).reshape(8, -1).astype(np.int64)


def pick8(x, idx, run):
    r = np.arange(len(x))
    return x[r[:, None], idx[r % (8 * run) // run]]


E2M1 = np.array([0.0, 0.5, 1.0, 1.5, 2.0, 3.0, 4.0, 6.0, -0.0, -0.5, -1.0, -1.5, -2.0, -3.0, -4.0, -6.0])


def pack_weight(w, fmt):
    k, n = w.shape
    w = f64(np.asarray(w, np.float32).astype(ml_dtypes.bfloat16)).reshape(k // 32, 32, n)
    amax = np.abs(w).max(1)
    if fmt == "e4m3":
        byte = np.frexp(amax)[1] - 1 + 127 - 7
    else:
        mant, ex = np.frexp(amax / 6.0)
        byte = np.where(mant > 0.5, ex, ex - 1) + 127
    byte = np.clip(np.where(amax > 0, byte, 1), 1, 254)
    scaled = (w * np.exp2(127.0 - byte)[:, None, :]).reshape(k, n).astype(np.float32)
    by_word = np.ascontiguousarray(scaled.reshape(k // 512, 128, 4, n).transpose(0, 1, 3, 2))
    if fmt == "e4m3":
        words = by_word.astype(ml_dtypes.float8_e4m3fn).view(np.uint8)
    else:
        c = by_word.astype(ml_dtypes.float4_e2m1fn).view(np.uint8) & 0xF
        words = (c[..., 0::2] | (c[..., 1::2] << 4)).reshape(k // 512, 128, 2 * n)
    return np.ascontiguousarray(words), np.ascontiguousarray(byte.astype(np.uint8).reshape(k // 512, 16, n))


def unpack_weight(words, scales, fmt):
    g, _, n = scales.shape
    words = np.ascontiguousarray(words).reshape(g, 128, n, -1)
    if fmt == "e4m3":
        vals = words.view(ml_dtypes.float8_e4m3fn).astype(np.float64)
    else:
        nib = np.empty((g, 128, n, 4), np.uint8)
        nib[..., 0::2] = words & 0xF
        nib[..., 1::2] = words >> 4
        vals = E2M1[nib]
    vals = vals * np.repeat(np.exp2(scales.astype(np.float64) - 127.0), 8, axis=1)[..., None]
    return vals.transpose(0, 1, 3, 2).reshape(g * 512, n)


def bf(x):
    return np.asarray(x, np.float32).astype(ml_dtypes.bfloat16)


def planes(Y):
    r, m = Y.shape
    b = f64(bf(Y)).reshape(r // 32, 32, m)
    amax = np.abs(b).max(1)
    byte = np.clip(np.where(amax > 0, np.frexp(amax)[1] - 1 + 127 - 7, 1), 1, 254)
    codes = (b * np.exp2(127.0 - byte)[:, None, :]).reshape(r, m).astype(np.float32).astype(ml_dtypes.float8_e4m3fn).view(np.uint8)
    words = codes.reshape(r // 512, 128, 4, m).transpose(0, 1, 3, 2)
    return np.ascontiguousarray(words), np.ascontiguousarray(byte.astype(np.uint8).reshape(r // 512, 16, m))


K, T, J, R, N, V = 512, 1024, 512, 512, 512, 512


def setup_inputs():
    n = np.random.standard_normal
    idx = np.random.permutation(T)[:J]
    idx2 = np.stack([np.random.randint(0, V, J) for _ in range(8)])
    fk = mx_kscale(K)
    fr = mx_kscale(R)
    xtp = pack_weight(n((K, T)) / fk[:, None], "e2m1")
    wap = pack_weight(n((K, R)) * 1 / np.sqrt(K) * fk[:, None] * fr, "e4m3")
    wbp = pack_weight(n((R, N)) * 1 / np.sqrt(R) / fr[:, None], "e2m1")
    return {
        "xt_words": xtp[0],
        "xt_scales": xtp[1],
        "wa_words": wap[0],
        "wa_scales": wap[1],
        "tb": (n((R, V)) * 0.7 * fr[:, None]).astype(np.float32),
        "wb_words": wbp[0],
        "wb_scales": wbp[1],
        "offs": striped(idx),
        "offs2": striped8(idx2),
    }


def reference(xt_words, xt_scales, wa_words, wa_scales, tb, wb_words, wb_scales, offs, offs2):
    idx = unstriped(offs)
    idx2 = unstriped8(offs2)
    xtu = unpack_weight(xt_words, xt_scales, "e2m1")
    wau = unpack_weight(wa_words, wa_scales, "e4m3")
    wbu = unpack_weight(wb_words, wb_scales, "e2m1")
    xtidxg = xtu[:, idx]
    a = wau.T @ xtidxg
    hid = np.maximum(a, 0.0) + pick8(f64(tb), idx2, 64)
    hidq = mxq(hid, 0, "e4m3")
    y = wbu.T @ hidq
    words, scales = planes(y)
    return y, words, scales

@@ -1,0 +1,180 @@
+from contextlib import ExitStack
+
+import concourse.mybir as mybir
+from concourse.masks import make_identity
+
+K, T, J, R, N, V = 512, 1024, 512, 512, 512, 512
+FLOPS = 2 * K * R * J + 2 * R * N * J
+
+F32 = mybir.dt.float32
+BF16 = mybir.dt.bfloat16
+I32 = mybir.dt.int32
+U32 = mybir.dt.uint32
+U16 = mybir.dt.uint16
+U8 = mybir.dt.uint8
+FP8X4 = mybir.dt.float8_e4m3fn_x4
+FP4X4 = mybir.dt.float4_e2m1fn_x4
+RELU = mybir.ActivationFunctionType.Relu
+ADD = mybir.AluOpType.add
+
+P = 128
+PACK = 4
+CHUNK = 128
+CHUNKS = J // CHUNK
+
+
+def load_scale_rows(queue, plane, rows):
+    for q in range(4):
+        queue.dma_start(out=plane[32 * q : 32 * q + 4, :].bitcast(I32), in_=rows[4 * q : 4 * q + 4, :].bitcast(I32))
+
+
+def tile_moe_expert_hidden_own_entries_pl_kernel(
+    tc, xt_words, xt_scales, wa_words, wa_scales, tb, wb_words, wb_scales, offs, offs2, out_0, out_1, out_2
+):
+    nc = tc.nc
+    with ExitStack() as ctx:
+        keep = ctx.enter_context(tc.tile_pool(name="keep", bufs=1))
+        psum = ctx.enter_context(tc.psum_pool(name="psum", bufs=1))
+
+        token_list = keep.tile([P, J // 16], U16)
+        entry_lists = keep.tile([P, J // 16], U16)
+        x_words = keep.tile([P, 2 * T], U8, align_bytes=64)
+        x_plane = keep.tile([P, T], U8, align_bytes=64)
+        wa_codes = keep.tile([P, R], U32, align_bytes=64)
+        wa_plane = keep.tile([P, R], U8, align_bytes=64)
+        wb_raw = keep.tile([P, 2 * N], U8, align_bytes=64)
+        wb_raw_plane = keep.tile([P, N], U8, align_bytes=64)
+        table = [keep.tile([P, V], F32, name=f"table{t}", align_bytes=64) for t in range(PACK)]
+        ident = keep.tile([P, P], F32)
+
+        nc.vector.memset(x_plane[:].bitcast(I32), 0)
+        nc.vector.memset(wa_plane[:].bitcast(I32), 0)
+        nc.vector.memset(wb_raw_plane[:].bitcast(I32), 0)
+        make_identity(nc, ident[:])
+
+        tb_rows = tb.rearrange("(p t) v -> t p v", t=PACK)
+        nc.sync.dma_start(token_list[:], offs)
+        nc.sync.dma_start(out=x_words[:].bitcast(I32), in_=xt_words[0].bitcast(I32))
+        load_scale_rows(nc.scalar, x_plane, xt_scales[0])
+        nc.sync.dma_start(entry_lists[:], offs2)
+        nc.sync.dma_start(out=table[0][:], in_=tb_rows[0])
+        nc.sync.dma_start(out=wa_codes[:].bitcast(I32), in_=wa_words[0].rearrange("p n t -> p (n t)").bitcast(I32))
+        load_scale_rows(nc.sync, wa_plane, wa_scales[0])
+        for t in range(1, PACK):
+            nc.sync.dma_start(out=table[t][:], in_=tb_rows[t])
+        nc.sync.dma_start(out=wb_raw[:].bitcast(I32), in_=wb_words[0].bitcast(I32))
+        load_scale_rows(nc.sync, wb_raw_plane, wb_scales[0])
+
+        xg_words = keep.tile([P, 2 * J], U8, align_bytes=64)
+        xg_plane = keep.tile([P, J], U8, align_bytes=64)
+        nc.vector.tensor_copy(out=xg_words[:].bitcast(U16), in_=x_words[:].bitcast(U16).indirect(token_list[:]))
+        nc.vector.tensor_copy(out=xg_plane[:], in_=x_plane[:].indirect(token_list[:]))
+
+        relu_a = []
+        for c in range(CHUNKS):
+            a_rows = psum.tile([P, R], F32, tag="a_rows", bufs=2, name=f"a_rows{c}")
+            nc.tensor.matmul_mx(
+                out=a_rows[:],
+                lhsT=xg_words[:, 2 * CHUNK * c : 2 * CHUNK * (c + 1)].bitcast(FP4X4),
+                lhsT_scale=xg_plane[:, CHUNK * c : CHUNK * (c + 1)],
+                rhs=wa_codes[:].bitcast(FP8X4),
+                rhs_scale=wa_plane[:],
+                start=True,
+                stop=True,
+            )
+            dealt = keep.tile([P, PACK, P], F32, name=f"dealt{c}")
+            nc.scalar.activation(out=dealt[:], in_=a_rows[:].rearrange("j (m t) -> j t m", t=PACK), func=RELU)
+            turned = psum.tile([P, PACK, CHUNK], F32, name=f"turned{c}")
+            for t in range(PACK):
+                nc.tensor.transpose(turned[:, t, :], dealt[:, t, :], ident[:])
+            relu_a.append(turned)
+
+        wb_codes = keep.tile([P, 2 * N], U8, align_bytes=64)
+        wb_plane = keep.tile([P, N], U8, align_bytes=64)
+        y_codes = keep.tile([P, J], U32, align_bytes=64)
+        y_plane = keep.tile([P, J], U8, align_bytes=64)
+        out_rows = out_0.rearrange("(p t) j -> p t j", t=PACK)
+        out_words = out_1[0].rearrange("p c t -> p (c t)").bitcast(I32)
+
+        def gather_entries(c):
+            entries = keep.tile([P, PACK, CHUNK], F32, tag="entries", bufs=2, name=f"entries{c}")
+            cols = slice(c * CHUNK // 16, (c + 1) * CHUNK // 16)
+            for t in range(PACK):
+                nc.vector.tensor_copy(out=entries[:, t, :], in_=table[t][:].indirect(entry_lists[:, cols]))
+            return entries
+
+        def add_entries(c, entries):
+            hid = keep.tile([P, CHUNK, PACK], BF16, name=f"hid{c}", align_bytes=64)
+            nc.vector.tensor_tensor(
+                out=hid[:].rearrange("p (b i) t -> p b t i", i=4),
+                in0=relu_a[c][:].rearrange("p t (b i) -> p b t i", i=4),
+                in1=entries[:].rearrange("p t (b i) -> p b t i", i=4),
+                op=ADD,
+            )
+            return hid
+
+        def second_layer(c, hid):
+            cols = slice(c * CHUNK, (c + 1) * CHUNK)
+            hid_codes = keep.tile([P, CHUNK], U32, name=f"hid_codes{c}", align_bytes=64)
+            hid_plane = keep.tile([P, CHUNK], U8, name=f"hid_plane{c}", align_bytes=64)
+            nc.vector.quantize_mx(
+                out=hid_codes[:].bitcast(FP8X4), scales=hid_plane[:], in_=hid[:].rearrange("p j t -> p (j t)")
+            )
+            y = psum.tile([P, PACK, CHUNK], F32, tag="y", bufs=2, name=f"y{c}")
+            for t in range(PACK):
+                nc.tensor.matmul_mx(
+                    out=y[:, t, :],
+                    lhsT=wb_codes[:, 2 * P * t : 2 * P * (t + 1)].bitcast(FP4X4),
+                    lhsT_scale=wb_plane[:, P * t : P * (t + 1)],
+                    rhs=hid_codes[:].bitcast(FP8X4),
+                    rhs_scale=hid_plane[:],
+                    start=True,
+                    stop=True,
+                )
+            y_sb = keep.tile([P, PACK, CHUNK], F32, name=f"y_sb{c}")
+            nc.scalar.copy(out=y_sb[:], in_=y[:])
+            nc.sync.dma_start(out=out_rows[:, :, cols], in_=y_sb[:])
+            y_bf = keep.tile([P, CHUNK, PACK], BF16, name=f"y_bf{c}", align_bytes=64)
+            if c < CHUNKS - 1:
+                nc.scalar.copy(out=y_bf[:], in_=y[:].rearrange("p t j -> p j t"))
+            else:
+                nc.vector.tensor_copy(
+                    out=y_bf[:].rearrange("p (b i) t -> p b t i", i=4), in_=y_sb[:].rearrange("p t (b i) -> p b t i", i=4)
+                )
+            return y_bf
+
+        def quantise_result(c, y_bf):
+            cols = slice(c * CHUNK, (c + 1) * CHUNK)
+            nc.vector.quantize_mx(
+                out=y_codes[:, cols].bitcast(FP8X4), scales=y_plane[:, cols], in_=y_bf[:].rearrange("p j t -> p (j t)")
+            )
+            nc.sync.dma_start(out=out_words[:, cols], in_=y_codes[:, cols].bitcast(I32))
+
+        entries0 = gather_entries(0)
+        entries1 = gather_entries(1)
+        nc.vector.tensor_copy(
+            out=wb_codes[:].bitcast(U16).rearrange("p (t m) -> p t m", t=PACK),
+            in_=wb_raw[:].bitcast(U16).rearrange("p (m t) -> p t m", t=PACK),
+        )
+        nc.vector.tensor_copy(
+            out=wb_plane[:].rearrange("p (t m) -> p t m", t=PACK),
+            in_=wb_raw_plane[:].rearrange("p (m t) -> p t m", t=PACK),
+        )
+        hid0 = add_entries(0, entries0)
+        hid1 = add_entries(1, entries1)
+        y0 = second_layer(0, hid0)
+        y1 = second_layer(1, hid1)
+        hid2 = add_entries(2, gather_entries(2))
+        entries3 = gather_entries(3)
+        y2 = second_layer(2, hid2)
+        hid3 = add_entries(3, entries3)
+        quantise_result(0, y0)
+        quantise_result(1, y1)
+        y3 = second_layer(3, hid3)
+        quantise_result(2, y2)
+        quantise_result(3, y3)
+        for q in range(4):
+            queue = nc.sync if q % 2 else nc.scalar
+            queue.dma_start(
+                out=out_2[0, 4 * q : 4 * q + 4, :].bitcast(I32), in_=y_plane[32 * q : 32 * q + 4, :].bitcast(I32)
+            )

@@ -47,15 +47,15 @@ def tile_moe_expert_hidden_own_entries_pl_kernel(
         table = [keep.tile([P, V], F32, name=f"table{t}", align_bytes=64) for t in range(PACK)]
         ident = keep.tile([P, P], F32)
 
-        nc.vector.memset(x_plane[:].bitcast(I32), 0)
-        nc.vector.memset(wa_plane[:].bitcast(I32), 0)
-        nc.vector.memset(wb_raw_plane[:].bitcast(I32), 0)
+        nc.gpsimd.memset(x_plane[:].bitcast(I32), 0)
+        nc.gpsimd.memset(wa_plane[:].bitcast(I32), 0)
+        nc.gpsimd.memset(wb_raw_plane[:].bitcast(I32), 0)
         make_identity(nc, ident[:])
 
         tb_rows = tb.rearrange("(p t) v -> t p v", t=PACK)
         nc.sync.dma_start(token_list[:], offs)
         nc.sync.dma_start(out=x_words[:].bitcast(I32), in_=xt_words[0].bitcast(I32))
-        load_scale_rows(nc.scalar, x_plane, xt_scales[0])
+        load_scale_rows(nc.sync, x_plane, xt_scales[0])
         nc.sync.dma_start(entry_lists[:], offs2)
         nc.sync.dma_start(out=table[0][:], in_=tb_rows[0])
         nc.sync.dma_start(out=wa_codes[:].bitcast(I32), in_=wa_words[0].rearrange("p n t -> p (n t)").bitcast(I32))
@@ -67,8 +67,8 @@ def tile_moe_expert_hidden_own_entries_pl_kernel(
 
         xg_words = keep.tile([P, 2 * J], U8, align_bytes=64)
         xg_plane = keep.tile([P, J], U8, align_bytes=64)
-        nc.vector.tensor_copy(out=xg_words[:].bitcast(U16), in_=x_words[:].bitcast(U16).indirect(token_list[:]))
         nc.vector.tensor_copy(out=xg_plane[:], in_=x_plane[:].indirect(token_list[:]))
+        nc.vector.tensor_copy(out=xg_words[:].bitcast(U16), in_=x_words[:].bitcast(U16).indirect(token_list[:]))
 
         relu_a = []
         for c in range(CHUNKS):
@@ -96,62 +96,68 @@ def tile_moe_expert_hidden_own_entries_pl_kernel(
         out_rows = out_0.rearrange("(p t) j -> p t j", t=PACK)
         out_words = out_1[0].rearrange("p c t -> p (c t)").bitcast(I32)
 
-        def gather_entries(c):
-            entries = keep.tile([P, PACK, CHUNK], F32, tag="entries", bufs=2, name=f"entries{c}")
-            cols = slice(c * CHUNK // 16, (c + 1) * CHUNK // 16)
-            for t in range(PACK):
-                nc.vector.tensor_copy(out=entries[:, t, :], in_=table[t][:].indirect(entry_lists[:, cols]))
-            return entries
+        entries = keep.tile([P, PACK, 2 * CHUNK], F32)
+        hid = keep.tile([P, J, PACK], BF16, align_bytes=64)
+        hid_codes = keep.tile([P, J], U32, align_bytes=64)
+        hid_plane = keep.tile([P, J], U8, align_bytes=64)
+        y_bf = keep.tile([P, J, PACK], BF16, align_bytes=64)
 
-        def add_entries(c, entries):
-            hid = keep.tile([P, CHUNK, PACK], BF16, name=f"hid{c}", align_bytes=64)
+        def slots(c0, c1):
+            return slice(c0 * CHUNK, c1 * CHUNK)
+
+        def gather_entries(c0, c1):
+            for t in range(PACK):
+                nc.vector.tensor_copy(
+                    out=entries[:, t, slots(c0 % 2, c0 % 2 + c1 - c0)],
+                    in_=table[t][:].indirect(entry_lists[:, c0 * CHUNK // 16 : c1 * CHUNK // 16]),
+                )
+
+        def add_entries(c):
             nc.vector.tensor_tensor(
-                out=hid[:].rearrange("p (b i) t -> p b t i", i=4),
-                in0=relu_a[c][:].rearrange("p t (b i) -> p b t i", i=4),
-                in1=entries[:].rearrange("p t (b i) -> p b t i", i=4),
+                out=hid[:, slots(c, c + 1), :].rearrange("p (b i) t -> p b t i", i=2),
+                in0=relu_a[c][:].rearrange("p t (b i) -> p b t i", i=2),
+                in1=entries[:, :, slots(c % 2, c % 2 + 1)].rearrange("p t (b i) -> p b t i", i=2),
                 op=ADD,
             )
-            return hid
 
-        def second_layer(c, hid):
-            cols = slice(c * CHUNK, (c + 1) * CHUNK)
-            hid_codes = keep.tile([P, CHUNK], U32, name=f"hid_codes{c}", align_bytes=64)
-            hid_plane = keep.tile([P, CHUNK], U8, name=f"hid_plane{c}", align_bytes=64)
+        def quantise(codes, plane, values, c0, c1):
+            cols = slots(c0, c1)
             nc.vector.quantize_mx(
-                out=hid_codes[:].bitcast(FP8X4), scales=hid_plane[:], in_=hid[:].rearrange("p j t -> p (j t)")
+                out=codes[:, cols].bitcast(FP8X4),
+                scales=plane[:, cols],
+                in_=values[:, cols, :].rearrange("p j t -> p (j t)"),
             )
+
+        def second_layer(c):
+            cols = slots(c, c + 1)
             y = psum.tile([P, PACK, CHUNK], F32, tag="y", bufs=2, name=f"y{c}")
             for t in range(PACK):
                 nc.tensor.matmul_mx(
                     out=y[:, t, :],
                     lhsT=wb_codes[:, 2 * P * t : 2 * P * (t + 1)].bitcast(FP4X4),
                     lhsT_scale=wb_plane[:, P * t : P * (t + 1)],
-                    rhs=hid_codes[:].bitcast(FP8X4),
-                    rhs_scale=hid_plane[:],
+                    rhs=hid_codes[:, cols].bitcast(FP8X4),
+                    rhs_scale=hid_plane[:, cols],
                     start=True,
                     stop=True,
                 )
             y_sb = keep.tile([P, PACK, CHUNK], F32, name=f"y_sb{c}")
-            nc.scalar.copy(out=y_sb[:], in_=y[:])
-            nc.sync.dma_start(out=out_rows[:, :, cols], in_=y_sb[:])
-            y_bf = keep.tile([P, CHUNK, PACK], BF16, name=f"y_bf{c}", align_bytes=64)
             if c < CHUNKS - 1:
-                nc.scalar.copy(out=y_bf[:], in_=y[:].rearrange("p t j -> p j t"))
+                nc.scalar.copy(out=y_sb[:], in_=y[:])
+                nc.sync.dma_start(out=out_rows[:, :, cols], in_=y_sb[:])
+                nc.scalar.copy(out=y_bf[:, cols, :], in_=y[:].rearrange("p t j -> p j t"))
             else:
-                nc.vector.tensor_copy(
-                    out=y_bf[:].rearrange("p (b i) t -> p b t i", i=4), in_=y_sb[:].rearrange("p t (b i) -> p b t i", i=4)
-                )
-            return y_bf
+                nc.scalar.copy(out=y_bf[:, cols, :], in_=y[:].rearrange("p t j -> p j t"))
+                for u in range(2):
+                    pair = slice(2 * u, 2 * u + 2)
+                    nc.scalar.copy(out=y_sb[:, pair, :], in_=y[:, pair, :])
+                    nc.sync.dma_start(out=out_rows[:, pair, cols], in_=y_sb[:, pair, :])
 
-        def quantise_result(c, y_bf):
-            cols = slice(c * CHUNK, (c + 1) * CHUNK)
-            nc.vector.quantize_mx(
-                out=y_codes[:, cols].bitcast(FP8X4), scales=y_plane[:, cols], in_=y_bf[:].rearrange("p j t -> p (j t)")
-            )
-            nc.sync.dma_start(out=out_words[:, cols], in_=y_codes[:, cols].bitcast(I32))
+        def quantise_result(c0, c1):
+            quantise(y_codes, y_plane, y_bf, c0, c1)
+            nc.sync.dma_start(out=out_words[:, slots(c0, c1)], in_=y_codes[:, slots(c0, c1)].bitcast(I32))
 
-        entries0 = gather_entries(0)
-        entries1 = gather_entries(1)
+        gather_entries(0, 2)
         nc.vector.tensor_copy(
             out=wb_codes[:].bitcast(U16).rearrange("p (t m) -> p t m", t=PACK),
             in_=wb_raw[:].bitcast(U16).rearrange("p (m t) -> p t m", t=PACK),
@@ -160,19 +166,22 @@ def tile_moe_expert_hidden_own_entries_pl_kernel(
             out=wb_plane[:].rearrange("p (t m) -> p t m", t=PACK),
             in_=wb_raw_plane[:].rearrange("p (m t) -> p t m", t=PACK),
         )
-        hid0 = add_entries(0, entries0)
-        hid1 = add_entries(1, entries1)
-        y0 = second_layer(0, hid0)
-        y1 = second_layer(1, hid1)
-        hid2 = add_entries(2, gather_entries(2))
-        entries3 = gather_entries(3)
-        y2 = second_layer(2, hid2)
-        hid3 = add_entries(3, entries3)
-        quantise_result(0, y0)
-        quantise_result(1, y1)
-        y3 = second_layer(3, hid3)
-        quantise_result(2, y2)
-        quantise_result(3, y3)
+        add_entries(0)
+        add_entries(1)
+        gather_entries(2, 3)
+        quantise(hid_codes, hid_plane, hid, 0, 2)
+        second_layer(0)
+        second_layer(1)
+        add_entries(2)
+        gather_entries(3, 4)
+        quantise(hid_codes, hid_plane, hid, 2, 3)
+        second_layer(2)
+        add_entries(3)
+        quantise_result(0, 2)
+        quantise(hid_codes, hid_plane, hid, 3, 4)
+        second_layer(3)
+        quantise_result(2, 3)
+        quantise_result(3, 4)
         for q in range(4):
             queue = nc.sync if q % 2 else nc.scalar
             queue.dma_start(

@@ -1,7 +1,6 @@
 from contextlib import ExitStack
 
 import concourse.mybir as mybir
-from concourse.masks import make_identity
 
 K, T, J, R, N, V = 512, 1024, 512, 512, 512, 512
 FLOPS = 2 * K * R * J + 2 * R * N * J
@@ -21,6 +20,7 @@ P = 128
 PACK = 4
 CHUNK = 128
 CHUNKS = J // CHUNK
+ENTRY_SLOTS = 3
 
 
 def load_scale_rows(queue, plane, rows):
@@ -43,14 +43,15 @@ def tile_moe_expert_hidden_own_entries_pl_kernel(
         wa_codes = keep.tile([P, R], U32, align_bytes=64)
         wa_plane = keep.tile([P, R], U8, align_bytes=64)
         wb_raw = keep.tile([P, 2 * N], U8, align_bytes=64)
-        wb_raw_plane = keep.tile([P, N], U8, align_bytes=64)
+        wb_raw_plane = keep.tile([P, N], U8, tag="staging", align_bytes=64)
         table = [keep.tile([P, V], F32, name=f"table{t}", align_bytes=64) for t in range(PACK)]
         ident = keep.tile([P, P], F32)
 
-        nc.gpsimd.memset(x_plane[:].bitcast(I32), 0)
-        nc.gpsimd.memset(wa_plane[:].bitcast(I32), 0)
-        nc.gpsimd.memset(wb_raw_plane[:].bitcast(I32), 0)
-        make_identity(nc, ident[:])
+        diagonal = keep.tile([P, P], I32)
+        for plane in (x_plane, wa_plane, wb_raw_plane):
+            nc.gpsimd.memset(plane[:].bitcast(I32), 0)
+        nc.gpsimd.iota(diagonal[:], pattern=[[1, P]], base=0, channel_multiplier=-1)
+        nc.vector.tensor_single_scalar(ident[:], diagonal[:], 0.0, mybir.AluOpType.is_equal)
 
         tb_rows = tb.rearrange("(p t) v -> t p v", t=PACK)
         nc.sync.dma_start(token_list[:], offs)
@@ -67,16 +68,19 @@ def tile_moe_expert_hidden_own_entries_pl_kernel(
 
         xg_words = keep.tile([P, 2 * J], U8, align_bytes=64)
         xg_plane = keep.tile([P, J], U8, align_bytes=64)
-        nc.vector.tensor_copy(out=xg_plane[:], in_=x_plane[:].indirect(token_list[:]))
         nc.vector.tensor_copy(out=xg_words[:].bitcast(U16), in_=x_words[:].bitcast(U16).indirect(token_list[:]))
+        nc.vector.tensor_copy(out=xg_plane[:], in_=x_plane[:].indirect(token_list[:]))
 
-        relu_a = []
+        def slots(c0, c1):
+            return slice(c0 * CHUNK, c1 * CHUNK)
+
+        turned = []
         for c in range(CHUNKS):
-            a_rows = psum.tile([P, R], F32, tag="a_rows", bufs=2, name=f"a_rows{c}")
+            a_rows = psum.tile([P, R], F32, tag="sums", bufs=4, name=f"a_rows{c}")
             nc.tensor.matmul_mx(
                 out=a_rows[:],
                 lhsT=xg_words[:, 2 * CHUNK * c : 2 * CHUNK * (c + 1)].bitcast(FP4X4),
-                lhsT_scale=xg_plane[:, CHUNK * c : CHUNK * (c + 1)],
+                lhsT_scale=xg_plane[:, slots(c, c + 1)],
                 rhs=wa_codes[:].bitcast(FP8X4),
                 rhs_scale=wa_plane[:],
                 start=True,
@@ -84,10 +88,9 @@ def tile_moe_expert_hidden_own_entries_pl_kernel(
             )
             dealt = keep.tile([P, PACK, P], F32, name=f"dealt{c}")
             nc.scalar.activation(out=dealt[:], in_=a_rows[:].rearrange("j (m t) -> j t m", t=PACK), func=RELU)
-            turned = psum.tile([P, PACK, CHUNK], F32, name=f"turned{c}")
+            turned.append(psum.tile([P, PACK, CHUNK], F32, name=f"turned{c}"))
             for t in range(PACK):
-                nc.tensor.transpose(turned[:, t, :], dealt[:, t, :], ident[:])
-            relu_a.append(turned)
+                nc.tensor.transpose(turned[c][:, t, :], dealt[:, t, :], ident[:])
 
         wb_codes = keep.tile([P, 2 * N], U8, align_bytes=64)
         wb_plane = keep.tile([P, N], U8, align_bytes=64)
@@ -95,42 +98,40 @@ def tile_moe_expert_hidden_own_entries_pl_kernel(
         y_plane = keep.tile([P, J], U8, align_bytes=64)
         out_rows = out_0.rearrange("(p t) j -> p t j", t=PACK)
         out_words = out_1[0].rearrange("p c t -> p (c t)").bitcast(I32)
-
-        entries = keep.tile([P, PACK, 2 * CHUNK], F32)
-        hid = keep.tile([P, J, PACK], BF16, align_bytes=64)
+        entries = keep.tile([P, PACK, ENTRY_SLOTS * CHUNK], F32)
         hid_codes = keep.tile([P, J], U32, align_bytes=64)
         hid_plane = keep.tile([P, J], U8, align_bytes=64)
-        y_bf = keep.tile([P, J, PACK], BF16, align_bytes=64)
+        hid = keep.tile([P, J, PACK], BF16, tag="staging", align_bytes=64)
+        y_sb = keep.tile([P, PACK, J], F32)
 
-        def slots(c0, c1):
-            return slice(c0 * CHUNK, c1 * CHUNK)
+        def entries_of(c, count=1):
+            return entries[:, :, slots(c % ENTRY_SLOTS, c % ENTRY_SLOTS + count)]
 
         def gather_entries(c0, c1):
             for t in range(PACK):
                 nc.vector.tensor_copy(
-                    out=entries[:, t, slots(c0 % 2, c0 % 2 + c1 - c0)],
+                    out=entries_of(c0, c1 - c0)[:, t, :],
                     in_=table[t][:].indirect(entry_lists[:, c0 * CHUNK // 16 : c1 * CHUNK // 16]),
                 )
 
         def add_entries(c):
             nc.vector.tensor_tensor(
                 out=hid[:, slots(c, c + 1), :].rearrange("p (b i) t -> p b t i", i=2),
-                in0=relu_a[c][:].rearrange("p t (b i) -> p b t i", i=2),
-                in1=entries[:, :, slots(c % 2, c % 2 + 1)].rearrange("p t (b i) -> p b t i", i=2),
+                in0=turned[c][:].rearrange("p t (b i) -> p b t i", i=2),
+                in1=entries_of(c).rearrange("p t (b i) -> p b t i", i=2),
                 op=ADD,
             )
 
         def quantise(codes, plane, values, c0, c1):
             cols = slots(c0, c1)
             nc.vector.quantize_mx(
-                out=codes[:, cols].bitcast(FP8X4),
-                scales=plane[:, cols],
-                in_=values[:, cols, :].rearrange("p j t -> p (j t)"),
+                out=codes[:, cols].bitcast(FP8X4), scales=plane[:, cols], in_=values.rearrange("p j t -> p (j t)")
             )
 
         def second_layer(c):
             cols = slots(c, c + 1)
-            y = psum.tile([P, PACK, CHUNK], F32, tag="y", bufs=2, name=f"y{c}")
+            quantise(hid_codes, hid_plane, hid[:, cols, :], c, c + 1)
+            y = psum.tile([P, PACK, CHUNK], F32, tag="sums", bufs=4, name=f"y{c}")
             for t in range(PACK):
                 nc.tensor.matmul_mx(
                     out=y[:, t, :],
@@ -141,23 +142,21 @@ def tile_moe_expert_hidden_own_entries_pl_kernel(
                     start=True,
                     stop=True,
                 )
-            y_sb = keep.tile([P, PACK, CHUNK], F32, name=f"y_sb{c}")
-            if c < CHUNKS - 1:
-                nc.scalar.copy(out=y_sb[:], in_=y[:])
-                nc.sync.dma_start(out=out_rows[:, :, cols], in_=y_sb[:])
-                nc.scalar.copy(out=y_bf[:, cols, :], in_=y[:].rearrange("p t j -> p j t"))
-            else:
-                nc.scalar.copy(out=y_bf[:, cols, :], in_=y[:].rearrange("p t j -> p j t"))
-                for u in range(2):
-                    pair = slice(2 * u, 2 * u + 2)
-                    nc.scalar.copy(out=y_sb[:, pair, :], in_=y[:, pair, :])
-                    nc.sync.dma_start(out=out_rows[:, pair, cols], in_=y_sb[:, pair, :])
+            return y
 
-        def quantise_result(c0, c1):
-            quantise(y_codes, y_plane, y_bf, c0, c1)
+        def store_sums(c, y, queue):
+            cols = slots(c, c + 1)
+            nc.scalar.copy(out=y_sb[:, :, cols], in_=y[:])
+            queue.dma_start(out=out_rows[:, :, cols], in_=y_sb[:, :, cols])
+
+        def round_sums(y, y_bf):
+            nc.scalar.copy(out=y_bf, in_=y[:].rearrange("p t j -> p j t"))
+
+        def store_words(c0, c1):
             nc.sync.dma_start(out=out_words[:, slots(c0, c1)], in_=y_codes[:, slots(c0, c1)].bitcast(I32))
 
         gather_entries(0, 2)
+        gather_entries(2, 3)
         nc.vector.tensor_copy(
             out=wb_codes[:].bitcast(U16).rearrange("p (t m) -> p t m", t=PACK),
             in_=wb_raw[:].bitcast(U16).rearrange("p (m t) -> p t m", t=PACK),
@@ -166,24 +165,30 @@ def tile_moe_expert_hidden_own_entries_pl_kernel(
             out=wb_plane[:].rearrange("p (t m) -> p t m", t=PACK),
             in_=wb_raw_plane[:].rearrange("p (m t) -> p t m", t=PACK),
         )
-        add_entries(0)
-        add_entries(1)
-        gather_entries(2, 3)
-        quantise(hid_codes, hid_plane, hid, 0, 2)
-        second_layer(0)
-        second_layer(1)
-        add_entries(2)
-        gather_entries(3, 4)
-        quantise(hid_codes, hid_plane, hid, 2, 3)
-        second_layer(2)
-        add_entries(3)
-        quantise_result(0, 2)
-        quantise(hid_codes, hid_plane, hid, 3, 4)
-        second_layer(3)
-        quantise_result(2, 3)
-        quantise_result(3, 4)
+        sums = []
+        for c in range(CHUNKS):
+            if c == ENTRY_SLOTS:
+                gather_entries(c, c + 1)
+            add_entries(c)
+            sums.append(second_layer(c))
+            if c < CHUNKS - 1:
+                store_sums(c, sums[c], nc.sync)
+        y_early = keep.tile([P, 3 * CHUNK, PACK], BF16, tag="staging", align_bytes=64)
+        round_sums(sums[0], y_early[:, slots(0, 1), :])
+        nc.vector.tensor_copy(
+            out=y_early[:, slots(1, 3), :].rearrange("p (b i) t -> p b t i", i=2),
+            in_=y_sb[:, :, slots(1, 3)].rearrange("p t (b i) -> p b t i", i=2),
+        )
+        quantise(y_codes, y_plane, y_early[:, slots(0, 1), :], 0, 1)
+        quantise(y_codes, y_plane, y_early[:, slots(1, 3), :], 1, 3)
+        store_words(0, 3)
+        y_last = keep.tile([P, CHUNK, PACK], BF16, align_bytes=64)
+        round_sums(sums[3], y_last[:])
+        quantise(y_codes, y_plane, y_last[:], 3, 4)
+        store_words(3, 4)
+        store_sums(3, sums[3], nc.scalar)
         for q in range(4):
-            queue = nc.sync if q % 2 else nc.scalar
+            queue = nc.sync if q < 2 else nc.scalar
             queue.dma_start(
                 out=out_2[0, 4 * q : 4 * q + 4, :].bitcast(I32), in_=y_plane[32 * q : 32 * q + 4, :].bitcast(I32)
             )

@@ -1,6 +1,7 @@
 from contextlib import ExitStack
 
 import concourse.mybir as mybir
+from concourse.masks import make_identity
 
 K, T, J, R, N, V = 512, 1024, 512, 512, 512, 512
 FLOPS = 2 * K * R * J + 2 * R * N * J
@@ -18,14 +19,35 @@ ADD = mybir.AluOpType.add
 
 P = 128
 PACK = 4
+FP4_WORD = 2
+QUADRANTS = 4
+LIST_ROWS = 16
 CHUNK = 128
 CHUNKS = J // CHUNK
-ENTRY_SLOTS = 3
+LAST = CHUNKS - 1
+ENTRY_CHUNKS = 3
+PSUM_ADD_CHUNK = 1
+SUM_BANKS = 4
 
 
-def load_scale_rows(queue, plane, rows):
-    for q in range(4):
-        queue.dma_start(out=plane[32 * q : 32 * q + 4, :].bitcast(I32), in_=rows[4 * q : 4 * q + 4, :].bitcast(I32))
+def plane_rows(plane, q):
+    return plane[32 * q : 32 * q + 4, :].bitcast(I32)
+
+
+def scale_rows(scales, q):
+    return scales[0, 4 * q : 4 * q + 4, :].bitcast(I32)
+
+
+def slots(c0, c1):
+    return slice(c0 * CHUNK, c1 * CHUNK)
+
+
+def by_slot_pairs(dealt):
+    return dealt.rearrange("p t (b i) -> p b t i", i=2)
+
+
+def words_by_slot_pairs(values):
+    return values.rearrange("p (b i) t -> p b t i", i=2)
 
 
 def tile_moe_expert_hidden_own_entries_pl_kernel(
@@ -36,127 +58,146 @@ def tile_moe_expert_hidden_own_entries_pl_kernel(
         keep = ctx.enter_context(tc.tile_pool(name="keep", bufs=1))
         psum = ctx.enter_context(tc.psum_pool(name="psum", bufs=1))
 
-        token_list = keep.tile([P, J // 16], U16)
-        entry_lists = keep.tile([P, J // 16], U16)
-        x_words = keep.tile([P, 2 * T], U8, align_bytes=64)
+        token_list = keep.tile([P, J // LIST_ROWS], U16)
+        entry_lists = keep.tile([P, J // LIST_ROWS], U16)
+        x_words = keep.tile([P, FP4_WORD * T], U8, align_bytes=64)
         x_plane = keep.tile([P, T], U8, align_bytes=64)
         wa_codes = keep.tile([P, R], U32, align_bytes=64)
         wa_plane = keep.tile([P, R], U8, align_bytes=64)
-        wb_raw = keep.tile([P, 2 * N], U8, align_bytes=64)
+        wb_raw = keep.tile([P, FP4_WORD * N], U8, align_bytes=64)
         wb_raw_plane = keep.tile([P, N], U8, tag="staging", align_bytes=64)
         table = [keep.tile([P, V], F32, name=f"table{t}", align_bytes=64) for t in range(PACK)]
         ident = keep.tile([P, P], F32)
 
-        diagonal = keep.tile([P, P], I32)
         for plane in (x_plane, wa_plane, wb_raw_plane):
             nc.gpsimd.memset(plane[:].bitcast(I32), 0)
-        nc.gpsimd.iota(diagonal[:], pattern=[[1, P]], base=0, channel_multiplier=-1)
-        nc.vector.tensor_single_scalar(ident[:], diagonal[:], 0.0, mybir.AluOpType.is_equal)
+        make_identity(nc, ident[:])
+
+        def load_plane(plane, scales):
+            for q in range(QUADRANTS):
+                nc.sync.dma_start(out=plane_rows(plane, q), in_=scale_rows(scales, q))
 
         tb_rows = tb.rearrange("(p t) v -> t p v", t=PACK)
         nc.sync.dma_start(token_list[:], offs)
         nc.sync.dma_start(out=x_words[:].bitcast(I32), in_=xt_words[0].bitcast(I32))
-        load_scale_rows(nc.sync, x_plane, xt_scales[0])
+        load_plane(x_plane, xt_scales)
         nc.sync.dma_start(entry_lists[:], offs2)
         nc.sync.dma_start(out=table[0][:], in_=tb_rows[0])
         nc.sync.dma_start(out=wa_codes[:].bitcast(I32), in_=wa_words[0].rearrange("p n t -> p (n t)").bitcast(I32))
-        load_scale_rows(nc.sync, wa_plane, wa_scales[0])
+        load_plane(wa_plane, wa_scales)
         for t in range(1, PACK):
             nc.sync.dma_start(out=table[t][:], in_=tb_rows[t])
         nc.sync.dma_start(out=wb_raw[:].bitcast(I32), in_=wb_words[0].bitcast(I32))
-        load_scale_rows(nc.sync, wb_raw_plane, wb_scales[0])
+        load_plane(wb_raw_plane, wb_scales)
 
-        xg_words = keep.tile([P, 2 * J], U8, align_bytes=64)
+        xg_words = keep.tile([P, FP4_WORD * J], U8, align_bytes=64)
         xg_plane = keep.tile([P, J], U8, align_bytes=64)
         nc.vector.tensor_copy(out=xg_words[:].bitcast(U16), in_=x_words[:].bitcast(U16).indirect(token_list[:]))
         nc.vector.tensor_copy(out=xg_plane[:], in_=x_plane[:].indirect(token_list[:]))
 
-        def slots(c0, c1):
-            return slice(c0 * CHUNK, c1 * CHUNK)
-
         turned = []
+        relu_rows = []
         for c in range(CHUNKS):
-            a_rows = psum.tile([P, R], F32, tag="sums", bufs=4, name=f"a_rows{c}")
+            a_rows = psum.tile([P, R], F32, tag="sums", bufs=SUM_BANKS, name=f"a_rows{c}")
             nc.tensor.matmul_mx(
                 out=a_rows[:],
-                lhsT=xg_words[:, 2 * CHUNK * c : 2 * CHUNK * (c + 1)].bitcast(FP4X4),
+                lhsT=xg_words[:, FP4_WORD * CHUNK * c : FP4_WORD * CHUNK * (c + 1)].bitcast(FP4X4),
                 lhsT_scale=xg_plane[:, slots(c, c + 1)],
                 rhs=wa_codes[:].bitcast(FP8X4),
                 rhs_scale=wa_plane[:],
                 start=True,
                 stop=True,
             )
-            dealt = keep.tile([P, PACK, P], F32, name=f"dealt{c}")
-            nc.scalar.activation(out=dealt[:], in_=a_rows[:].rearrange("j (m t) -> j t m", t=PACK), func=RELU)
+            relu_rows.append(keep.tile([P, PACK, P], F32, name=f"relu_rows{c}"))
+            nc.scalar.activation(out=relu_rows[c][:], in_=a_rows[:].rearrange("j (m t) -> j t m", t=PACK), func=RELU)
             turned.append(psum.tile([P, PACK, CHUNK], F32, name=f"turned{c}"))
-            for t in range(PACK):
-                nc.tensor.transpose(turned[c][:, t, :], dealt[:, t, :], ident[:])
+            if c != PSUM_ADD_CHUNK:
+                for t in range(PACK):
+                    nc.tensor.transpose(turned[c][:, t, :], relu_rows[c][:, t, :], ident[:])
 
-        wb_codes = keep.tile([P, 2 * N], U8, align_bytes=64)
+        wb_codes = keep.tile([P, FP4_WORD * N], U8, align_bytes=64)
         wb_plane = keep.tile([P, N], U8, align_bytes=64)
         y_codes = keep.tile([P, J], U32, align_bytes=64)
         y_plane = keep.tile([P, J], U8, align_bytes=64)
         out_rows = out_0.rearrange("(p t) j -> p t j", t=PACK)
         out_words = out_1[0].rearrange("p c t -> p (c t)").bitcast(I32)
-        entries = keep.tile([P, PACK, ENTRY_SLOTS * CHUNK], F32)
+        entries = keep.tile([P, PACK, ENTRY_CHUNKS * CHUNK], F32)
         hid_codes = keep.tile([P, J], U32, align_bytes=64)
         hid_plane = keep.tile([P, J], U8, align_bytes=64)
         hid = keep.tile([P, J, PACK], BF16, tag="staging", align_bytes=64)
-        y_sb = keep.tile([P, PACK, J], F32)
+        y_f32 = keep.tile([P, PACK, J], F32)
 
         def entries_of(c, count=1):
-            return entries[:, :, slots(c % ENTRY_SLOTS, c % ENTRY_SLOTS + count)]
+            return entries[:, :, slots(c % ENTRY_CHUNKS, c % ENTRY_CHUNKS + count)]
 
         def gather_entries(c0, c1):
+            columns = slice(c0 * CHUNK // LIST_ROWS, c1 * CHUNK // LIST_ROWS)
             for t in range(PACK):
                 nc.vector.tensor_copy(
-                    out=entries_of(c0, c1 - c0)[:, t, :],
-                    in_=table[t][:].indirect(entry_lists[:, c0 * CHUNK // 16 : c1 * CHUNK // 16]),
+                    out=entries_of(c0, c1 - c0)[:, t, :], in_=table[t][:].indirect(entry_lists[:, columns])
                 )
 
         def add_entries(c):
             nc.vector.tensor_tensor(
-                out=hid[:, slots(c, c + 1), :].rearrange("p (b i) t -> p b t i", i=2),
-                in0=turned[c][:].rearrange("p t (b i) -> p b t i", i=2),
-                in1=entries_of(c).rearrange("p t (b i) -> p b t i", i=2),
+                out=words_by_slot_pairs(hid[:, slots(c, c + 1), :]),
+                in0=by_slot_pairs(turned[c][:]),
+                in1=by_slot_pairs(entries_of(c)),
                 op=ADD,
             )
 
+        def add_entries_in_psum(c):
+            entry_rows = psum.tile([P, PACK, P], F32, tag="sums", bufs=SUM_BANKS, name="entry_rows")
+            for t in range(PACK):
+                nc.tensor.transpose(entry_rows[:, t, :], entries_of(c)[:, t, :], ident[:])
+            entry_rows_sb = keep.tile([P, PACK, P], F32)
+            nc.scalar.copy(out=entry_rows_sb[:], in_=entry_rows[:])
+            for t in range(PACK):
+                for term, first in ((relu_rows[c], True), (entry_rows_sb, False)):
+                    nc.tensor.matmul(
+                        turned[c][:, t, :],
+                        lhsT=term[:, t, :],
+                        rhs=ident[:],
+                        is_transpose=True,
+                        start=first,
+                        stop=not first,
+                    )
+            nc.scalar.copy(out=hid[:, slots(c, c + 1), :], in_=turned[c][:].rearrange("p t j -> p j t"))
+
         def quantise(codes, plane, values, c0, c1):
-            cols = slots(c0, c1)
             nc.vector.quantize_mx(
-                out=codes[:, cols].bitcast(FP8X4), scales=plane[:, cols], in_=values.rearrange("p j t -> p (j t)")
+                out=codes[:, slots(c0, c1)].bitcast(FP8X4),
+                scales=plane[:, slots(c0, c1)],
+                in_=values.rearrange("p j t -> p (j t)"),
             )
 
         def second_layer(c):
-            cols = slots(c, c + 1)
-            quantise(hid_codes, hid_plane, hid[:, cols, :], c, c + 1)
-            y = psum.tile([P, PACK, CHUNK], F32, tag="sums", bufs=4, name=f"y{c}")
+            quantise(hid_codes, hid_plane, hid[:, slots(c, c + 1), :], c, c + 1)
+            y = psum.tile([P, PACK, CHUNK], F32, tag="sums", bufs=SUM_BANKS, name=f"y{c}")
             for t in range(PACK):
                 nc.tensor.matmul_mx(
                     out=y[:, t, :],
-                    lhsT=wb_codes[:, 2 * P * t : 2 * P * (t + 1)].bitcast(FP4X4),
+                    lhsT=wb_codes[:, FP4_WORD * P * t : FP4_WORD * P * (t + 1)].bitcast(FP4X4),
                     lhsT_scale=wb_plane[:, P * t : P * (t + 1)],
-                    rhs=hid_codes[:, cols].bitcast(FP8X4),
-                    rhs_scale=hid_plane[:, cols],
+                    rhs=hid_codes[:, slots(c, c + 1)].bitcast(FP8X4),
+                    rhs_scale=hid_plane[:, slots(c, c + 1)],
                     start=True,
                     stop=True,
                 )
             return y
 
         def store_sums(c, y, queue):
-            cols = slots(c, c + 1)
-            nc.scalar.copy(out=y_sb[:, :, cols], in_=y[:])
-            queue.dma_start(out=out_rows[:, :, cols], in_=y_sb[:, :, cols])
+            nc.scalar.copy(out=y_f32[:, :, slots(c, c + 1)], in_=y[:])
+            queue.dma_start(out=out_rows[:, :, slots(c, c + 1)], in_=y_f32[:, :, slots(c, c + 1)])
 
-        def round_sums(y, y_bf):
-            nc.scalar.copy(out=y_bf, in_=y[:].rearrange("p t j -> p j t"))
+        def round_sums(y, y_bf16):
+            nc.scalar.copy(out=y_bf16, in_=y[:].rearrange("p t j -> p j t"))
 
         def store_words(c0, c1):
             nc.sync.dma_start(out=out_words[:, slots(c0, c1)], in_=y_codes[:, slots(c0, c1)].bitcast(I32))
 
         gather_entries(0, 2)
-        gather_entries(2, 3)
+        gather_entries(2, ENTRY_CHUNKS)
+
         nc.vector.tensor_copy(
             out=wb_codes[:].bitcast(U16).rearrange("p (t m) -> p t m", t=PACK),
             in_=wb_raw[:].bitcast(U16).rearrange("p (m t) -> p t m", t=PACK),
@@ -165,30 +206,35 @@ def tile_moe_expert_hidden_own_entries_pl_kernel(
             out=wb_plane[:].rearrange("p (t m) -> p t m", t=PACK),
             in_=wb_raw_plane[:].rearrange("p (m t) -> p t m", t=PACK),
         )
-        sums = []
-        for c in range(CHUNKS):
-            if c == ENTRY_SLOTS:
-                gather_entries(c, c + 1)
+
+        add_entries_in_psum(PSUM_ADD_CHUNK)
+        vector_early = [c for c in range(ENTRY_CHUNKS) if c != PSUM_ADD_CHUNK]
+        for c in vector_early:
             add_entries(c)
-            sums.append(second_layer(c))
-            if c < CHUNKS - 1:
-                store_sums(c, sums[c], nc.sync)
-        y_early = keep.tile([P, 3 * CHUNK, PACK], BF16, tag="staging", align_bytes=64)
+        sums = {}
+        for c in vector_early:
+            sums[c] = second_layer(c)
+            store_sums(c, sums[c], nc.sync)
+        gather_entries(LAST, CHUNKS)
+        sums[PSUM_ADD_CHUNK] = second_layer(PSUM_ADD_CHUNK)
+        store_sums(PSUM_ADD_CHUNK, sums[PSUM_ADD_CHUNK], nc.sync)
+        add_entries(LAST)
+        sums[LAST] = second_layer(LAST)
+
+        y_early = keep.tile([P, LAST * CHUNK, PACK], BF16, tag="staging", align_bytes=64)
         round_sums(sums[0], y_early[:, slots(0, 1), :])
         nc.vector.tensor_copy(
-            out=y_early[:, slots(1, 3), :].rearrange("p (b i) t -> p b t i", i=2),
-            in_=y_sb[:, :, slots(1, 3)].rearrange("p t (b i) -> p b t i", i=2),
+            out=words_by_slot_pairs(y_early[:, slots(1, LAST), :]), in_=by_slot_pairs(y_f32[:, :, slots(1, LAST)])
         )
         quantise(y_codes, y_plane, y_early[:, slots(0, 1), :], 0, 1)
-        quantise(y_codes, y_plane, y_early[:, slots(1, 3), :], 1, 3)
-        store_words(0, 3)
+        quantise(y_codes, y_plane, y_early[:, slots(1, LAST), :], 1, LAST)
+        store_words(0, LAST)
+
         y_last = keep.tile([P, CHUNK, PACK], BF16, align_bytes=64)
-        round_sums(sums[3], y_last[:])
-        quantise(y_codes, y_plane, y_last[:], 3, 4)
-        store_words(3, 4)
-        store_sums(3, sums[3], nc.scalar)
-        for q in range(4):
-            queue = nc.sync if q < 2 else nc.scalar
-            queue.dma_start(
-                out=out_2[0, 4 * q : 4 * q + 4, :].bitcast(I32), in_=y_plane[32 * q : 32 * q + 4, :].bitcast(I32)
-            )
+        round_sums(sums[LAST], y_last[:])
+        quantise(y_codes, y_plane, y_last[:], LAST, CHUNKS)
+        store_words(LAST, CHUNKS)
+        store_sums(LAST, sums[LAST], nc.scalar)
+        for q in range(QUADRANTS):
+            queue = nc.sync if q < QUADRANTS // 2 else nc.scalar
+            queue.dma_start(out=scale_rows(out_2, q), in_=plane_rows(y_plane, q))

from contextlib import ExitStack

import concourse.mybir as mybir
from concourse.masks import make_identity

K, T, J, R, N, V = 512, 1024, 512, 512, 512, 512
FLOPS = 2 * K * R * J + 2 * R * N * J

F32 = mybir.dt.float32
BF16 = mybir.dt.bfloat16
I32 = mybir.dt.int32
U32 = mybir.dt.uint32
U16 = mybir.dt.uint16
U8 = mybir.dt.uint8
FP8X4 = mybir.dt.float8_e4m3fn_x4
FP4X4 = mybir.dt.float4_e2m1fn_x4
RELU = mybir.ActivationFunctionType.Relu
ADD = mybir.AluOpType.add

P = 128
PACK = 4
FP4_WORD = 2
QUADRANTS = 4
LIST_ROWS = 16
CHUNK = 128
CHUNKS = J // CHUNK
LAST = CHUNKS - 1
ENTRY_CHUNKS = 3
PSUM_ADD_CHUNK = 1
SUM_BANKS = 4


def plane_rows(plane, q):
    return plane[32 * q : 32 * q + 4, :].bitcast(I32)


def scale_rows(scales, q):
    return scales[0, 4 * q : 4 * q + 4, :].bitcast(I32)


def slots(c0, c1):
    return slice(c0 * CHUNK, c1 * CHUNK)


def by_slot_pairs(dealt):
    return dealt.rearrange("p t (b i) -> p b t i", i=2)


def words_by_slot_pairs(values):
    return values.rearrange("p (b i) t -> p b t i", i=2)


def tile_moe_expert_hidden_own_entries_pl_kernel(
    tc, xt_words, xt_scales, wa_words, wa_scales, tb, wb_words, wb_scales, offs, offs2, out_0, out_1, out_2
):
    nc = tc.nc
    with ExitStack() as ctx:
        keep = ctx.enter_context(tc.tile_pool(name="keep", bufs=1))
        psum = ctx.enter_context(tc.psum_pool(name="psum", bufs=1))

        token_list = keep.tile([P, J // LIST_ROWS], U16)
        entry_lists = keep.tile([P, J // LIST_ROWS], U16)
        x_words = keep.tile([P, FP4_WORD * T], U8, align_bytes=64)
        x_plane = keep.tile([P, T], U8, align_bytes=64)
        wa_codes = keep.tile([P, R], U32, align_bytes=64)
        wa_plane = keep.tile([P, R], U8, align_bytes=64)
        wb_raw = keep.tile([P, FP4_WORD * N], U8, align_bytes=64)
        wb_raw_plane = keep.tile([P, N], U8, tag="staging", align_bytes=64)
        table = [keep.tile([P, V], F32, name=f"table{t}", align_bytes=64) for t in range(PACK)]
        ident = keep.tile([P, P], F32)

        for plane in (x_plane, wa_plane, wb_raw_plane):
            nc.gpsimd.memset(plane[:].bitcast(I32), 0)
        make_identity(nc, ident[:])

        def load_plane(plane, scales):
            for q in range(QUADRANTS):
                nc.sync.dma_start(out=plane_rows(plane, q), in_=scale_rows(scales, q))

        tb_rows = tb.rearrange("(p t) v -> t p v", t=PACK)
        nc.sync.dma_start(token_list[:], offs)
        nc.sync.dma_start(out=x_words[:].bitcast(I32), in_=xt_words[0].bitcast(I32))
        load_plane(x_plane, xt_scales)
        nc.sync.dma_start(entry_lists[:], offs2)
        nc.sync.dma_start(out=table[0][:], in_=tb_rows[0])
        nc.sync.dma_start(out=wa_codes[:].bitcast(I32), in_=wa_words[0].rearrange("p n t -> p (n t)").bitcast(I32))
        load_plane(wa_plane, wa_scales)
        for t in range(1, PACK):
            nc.sync.dma_start(out=table[t][:], in_=tb_rows[t])
        nc.sync.dma_start(out=wb_raw[:].bitcast(I32), in_=wb_words[0].bitcast(I32))
        load_plane(wb_raw_plane, wb_scales)

        xg_words = keep.tile([P, FP4_WORD * J], U8, align_bytes=64)
        xg_plane = keep.tile([P, J], U8, align_bytes=64)
        nc.vector.tensor_copy(out=xg_words[:].bitcast(U16), in_=x_words[:].bitcast(U16).indirect(token_list[:]))
        nc.vector.tensor_copy(out=xg_plane[:], in_=x_plane[:].indirect(token_list[:]))

        turned = []
        relu_rows = []
        for c in range(CHUNKS):
            a_rows = psum.tile([P, R], F32, tag="sums", bufs=SUM_BANKS, name=f"a_rows{c}")
            nc.tensor.matmul_mx(
                out=a_rows[:],
                lhsT=xg_words[:, FP4_WORD * CHUNK * c : FP4_WORD * CHUNK * (c + 1)].bitcast(FP4X4),
                lhsT_scale=xg_plane[:, slots(c, c + 1)],
                rhs=wa_codes[:].bitcast(FP8X4),
                rhs_scale=wa_plane[:],
                start=True,
                stop=True,
            )
            relu_rows.append(keep.tile([P, PACK, P], F32, name=f"relu_rows{c}"))
            nc.scalar.activation(out=relu_rows[c][:], in_=a_rows[:].rearrange("j (m t) -> j t m", t=PACK), func=RELU)
            turned.append(psum.tile([P, PACK, CHUNK], F32, name=f"turned{c}"))
            if c != PSUM_ADD_CHUNK:
                for t in range(PACK):
                    nc.tensor.transpose(turned[c][:, t, :], relu_rows[c][:, t, :], ident[:])

        wb_codes = keep.tile([P, FP4_WORD * N], U8, align_bytes=64)
        wb_plane = keep.tile([P, N], U8, align_bytes=64)
        y_codes = keep.tile([P, J], U32, align_bytes=64)
        y_plane = keep.tile([P, J], U8, align_bytes=64)
        out_rows = out_0.rearrange("(p t) j -> p t j", t=PACK)
        out_words = out_1[0].rearrange("p c t -> p (c t)").bitcast(I32)
        entries = keep.tile([P, PACK, ENTRY_CHUNKS * CHUNK], F32)
        hid_codes = keep.tile([P, J], U32, align_bytes=64)
        hid_plane = keep.tile([P, J], U8, align_bytes=64)
        hid = keep.tile([P, J, PACK], BF16, tag="staging", align_bytes=64)
        y_f32 = keep.tile([P, PACK, J], F32)

        def entries_of(c, count=1):
            return entries[:, :, slots(c % ENTRY_CHUNKS, c % ENTRY_CHUNKS + count)]

        def gather_entries(c0, c1):
            columns = slice(c0 * CHUNK // LIST_ROWS, c1 * CHUNK // LIST_ROWS)
            for t in range(PACK):
                nc.vector.tensor_copy(
                    out=entries_of(c0, c1 - c0)[:, t, :], in_=table[t][:].indirect(entry_lists[:, columns])
                )

        def add_entries(c):
            nc.vector.tensor_tensor(
                out=words_by_slot_pairs(hid[:, slots(c, c + 1), :]),
                in0=by_slot_pairs(turned[c][:]),
                in1=by_slot_pairs(entries_of(c)),
                op=ADD,
            )

        def add_entries_in_psum(c):
            entry_rows = psum.tile([P, PACK, P], F32, tag="sums", bufs=SUM_BANKS, name="entry_rows")
            for t in range(PACK):
                nc.tensor.transpose(entry_rows[:, t, :], entries_of(c)[:, t, :], ident[:])
            entry_rows_sb = keep.tile([P, PACK, P], F32)
            nc.scalar.copy(out=entry_rows_sb[:], in_=entry_rows[:])
            for t in range(PACK):
                for term, first in ((relu_rows[c], True), (entry_rows_sb, False)):
                    nc.tensor.matmul(
                        turned[c][:, t, :],
                        lhsT=term[:, t, :],
                        rhs=ident[:],
                        is_transpose=True,
                        start=first,
                        stop=not first,
                    )
            nc.scalar.copy(out=hid[:, slots(c, c + 1), :], in_=turned[c][:].rearrange("p t j -> p j t"))

        def quantise(codes, plane, values, c0, c1):
            nc.vector.quantize_mx(
                out=codes[:, slots(c0, c1)].bitcast(FP8X4),
                scales=plane[:, slots(c0, c1)],
                in_=values.rearrange("p j t -> p (j t)"),
            )

        def second_layer(c):
            quantise(hid_codes, hid_plane, hid[:, slots(c, c + 1), :], c, c + 1)
            y = psum.tile([P, PACK, CHUNK], F32, tag="sums", bufs=SUM_BANKS, name=f"y{c}")
            for t in range(PACK):
                nc.tensor.matmul_mx(
                    out=y[:, t, :],
                    lhsT=wb_codes[:, FP4_WORD * P * t : FP4_WORD * P * (t + 1)].bitcast(FP4X4),
                    lhsT_scale=wb_plane[:, P * t : P * (t + 1)],
                    rhs=hid_codes[:, slots(c, c + 1)].bitcast(FP8X4),
                    rhs_scale=hid_plane[:, slots(c, c + 1)],
                    start=True,
                    stop=True,
                )
            return y

        def store_sums(c, y, queue):
            nc.scalar.copy(out=y_f32[:, :, slots(c, c + 1)], in_=y[:])
            queue.dma_start(out=out_rows[:, :, slots(c, c + 1)], in_=y_f32[:, :, slots(c, c + 1)])

        def round_sums(y, y_bf16):
            nc.scalar.copy(out=y_bf16, in_=y[:].rearrange("p t j -> p j t"))

        def store_words(c0, c1):
            nc.sync.dma_start(out=out_words[:, slots(c0, c1)], in_=y_codes[:, slots(c0, c1)].bitcast(I32))

        gather_entries(0, 2)
        gather_entries(2, ENTRY_CHUNKS)

        nc.vector.tensor_copy(
            out=wb_codes[:].bitcast(U16).rearrange("p (t m) -> p t m", t=PACK),
            in_=wb_raw[:].bitcast(U16).rearrange("p (m t) -> p t m", t=PACK),
        )
        nc.vector.tensor_copy(
            out=wb_plane[:].rearrange("p (t m) -> p t m", t=PACK),
            in_=wb_raw_plane[:].rearrange("p (m t) -> p t m", t=PACK),
        )

        add_entries_in_psum(PSUM_ADD_CHUNK)
        vector_early = [c for c in range(ENTRY_CHUNKS) if c != PSUM_ADD_CHUNK]
        for c in vector_early:
            add_entries(c)
        sums = {}
        for c in vector_early:
            sums[c] = second_layer(c)
            store_sums(c, sums[c], nc.sync)
        gather_entries(LAST, CHUNKS)
        sums[PSUM_ADD_CHUNK] = second_layer(PSUM_ADD_CHUNK)
        store_sums(PSUM_ADD_CHUNK, sums[PSUM_ADD_CHUNK], nc.sync)
        add_entries(LAST)
        sums[LAST] = second_layer(LAST)

        y_early = keep.tile([P, LAST * CHUNK, PACK], BF16, tag="staging", align_bytes=64)
        round_sums(sums[0], y_early[:, slots(0, 1), :])
        nc.vector.tensor_copy(
            out=words_by_slot_pairs(y_early[:, slots(1, LAST), :]), in_=by_slot_pairs(y_f32[:, :, slots(1, LAST)])
        )
        quantise(y_codes, y_plane, y_early[:, slots(0, 1), :], 0, 1)
        quantise(y_codes, y_plane, y_early[:, slots(1, LAST), :], 1, LAST)
        store_words(0, LAST)

        y_last = keep.tile([P, CHUNK, PACK], BF16, align_bytes=64)
        round_sums(sums[LAST], y_last[:])
        quantise(y_codes, y_plane, y_last[:], LAST, CHUNKS)
        store_words(LAST, CHUNKS)
        store_sums(LAST, sums[LAST], nc.scalar)
        for q in range(QUADRANTS):
            queue = nc.sync if q < QUADRANTS // 2 else nc.scalar
            queue.dma_start(out=scale_rows(out_2, q), in_=plane_rows(y_plane, q))
